import numpy as np
import ml_dtypes


def mxq(x, axis, fmt="e4m3"):
    dtype, down = {"e4m3": (ml_dtypes.float8_e4m3fn, 7), "e5m2": (ml_dtypes.float8_e5m2, 14)}[fmt]
    v = np.moveaxis(np.asarray(x, np.float32).astype(ml_dtypes.bfloat16).astype(np.float64), axis, -1)
    blocks = v.reshape(v.shape[:-1] + (-1, 32))
    amax = np.abs(blocks).max(-1, keepdims=True)
    byte = np.maximum(np.where(amax > 0, np.frexp(amax)[1] - 1 + 127, 0) - down, 1)
    scale = np.exp2(byte - 127.0)
    codes = (blocks / scale).astype(np.float32).astype(dtype).astype(np.float64)
    return np.moveaxis((codes * scale).reshape(v.shape), -1, axis)


WIDE = False


def mx_kscale(k):
    if not WIDE:
        return np.ones(k)
    levels = np.array([10, -10, 5, -5, 0])
    if k % 512:
        return np.exp2(np.random.permutation(np.resize(levels, k // 32))).repeat(32)
    a = np.empty((k // 512, 16))
    for p in range(k // 512):
        a[p, :8] = np.random.permutation(np.resize(levels, 8))
        for g in range(8):
            far = levels[np.abs(levels - a[p, g]) >= 10]
            a[p, g + 8] = far[np.random.randint(len(far))]
    return np.exp2(a.ravel()).repeat(32)


BF16 = ml_dtypes.bfloat16


def bf(x):
    return np.asarray(x, np.float32).astype(BF16)


def f64(x):
    return np.asarray(x).astype(np.float64)

def planes(Y):
    n, m = Y.shape
    b = f64(bf(Y)).reshape(n // 32, 32, m)
    amax = np.abs(b).max(1)
    byte = np.clip(np.where(amax > 0, np.frexp(amax)[1] - 1 + 127 - 7, 1), 1, 254)
    codes = (b * np.exp2(127.0 - byte)[:, None, :]).reshape(n, m).astype(np.float32).astype(ml_dtypes.float8_e4m3fn).view(np.uint8)
    words = codes.reshape(n // 512, 128, 4, m).transpose(0, 1, 3, 2)
    return np.ascontiguousarray(words), np.ascontiguousarray(byte.astype(np.uint8).reshape(n // 512, 16, m))


G, K, S = 2048, 1024, 1024
SPAN = 4.0


def hermite_functions(x, count):
    h = [np.pi ** -0.25 * np.exp(-0.5 * x * x)]
    h.append(np.sqrt(2.0) * x * h[0])
    for n in range(1, count - 1):
        h.append(np.sqrt(2.0 / (n + 1)) * x * h[n] - np.sqrt(n / (n + 1)) * h[n - 1])
    return np.stack(h, axis=1)


def setup_inputs():
    s = mx_kscale(K)
    gaps = np.exp(np.random.randn(G + 1))
    x = SPAN * (2.0 * np.cumsum(gaps)[:-1] / gaps.sum() - 1.0)
    jac = 0.5 * (gaps[:-1] + gaps[1:]) / gaps.mean()
    basis = hermite_functions(x, K)
    coef_re = np.random.randn(K, S) / (2.0 * K) ** 0.25
    coef_im = np.random.randn(K, S) / (2.0 * K) ** 0.25
    return {
        "basis": bf(basis * s[None, :]),
        "coef_re": bf(coef_re / s[:, None]),
        "coef_im": bf(coef_im / s[:, None]),
        "jac": bf(jac),
    }


def reference(basis, coef_re, coef_im, jac):
    h = mxq(f64(basis), 1, "e4m3")
    re = h @ mxq(f64(coef_re), 0, "e4m3")
    im = h @ mxq(f64(coef_im), 0, "e4m3")
    y = (re * re + im * im) * f64(jac)[:, None]
    Y = y.reshape(G, S)
    words, scales = planes(Y)
    return y, words, scales

@@ -1,0 +1,253 @@
+from contextlib import ExitStack
+
+import concourse.mybir as mybir
+from concourse.masks import make_identity
+
+G, K, S = 2048, 1024, 1024
+FLOPS = 2 * 2 * G * K * S
+
+F32 = mybir.dt.float32
+BF16 = mybir.dt.bfloat16
+I32 = mybir.dt.int32
+U32 = mybir.dt.uint32
+U8 = mybir.dt.uint8
+FP8X4 = mybir.dt.float8_e4m3fn_x4
+SQUARE = mybir.ActivationFunctionType.Square
+ADD = mybir.AluOpType.add
+MULT = mybir.AluOpType.mult
+
+P = 128
+PACK = 4
+SPAN = P * PACK
+N = 512
+GROUPS = G // SPAN
+PASSES = K // SPAN
+HALVES = S // N
+STEPS = GROUPS * HALVES * PACK
+RUN = 4
+
+COEF_SCALAR_COLS = {0: (256, 256, 256, 256), 1: (0, 128, 128, 128)}
+CAST_SCALAR_COLS = (0, 0, 0, 0, 0, 192, 192, 192)
+TURN_AT = (3, 5)
+LAG = 1
+
+
+def tile_hermite_state_density_g2_kernel(tc, basis, coef_re, coef_im, jac, out_0, out_1, out_2):
+    nc = tc.nc
+    coefs = (coef_re, coef_im)
+
+    with ExitStack() as ctx:
+        keep = ctx.enter_context(tc.tile_pool(name="keep", bufs=1))
+        stage = ctx.enter_context(tc.tile_pool(name="stage", bufs=3))
+        squares = ctx.enter_context(tc.tile_pool(name="squares", bufs=8))
+        turn_psum = ctx.enter_context(tc.psum_pool(name="turn_psum", bufs=2))
+        acc_psum = ctx.enter_context(tc.psum_pool(name="acc_psum", bufs=3))
+        ctx.enter_context(tc.manual_schedule())
+
+        ident = keep.tile([P, P], F32)
+        jac_sb = keep.tile([P, GROUPS, PACK], BF16)
+        basis_raw = keep.tile([P, GROUPS, PACK, K], BF16)
+        coef_raw = keep.tile([P, HALVES, PASSES, 2, PACK, N], BF16)
+        basis_codes = keep.tile([P, GROUPS * PACK * PASSES * P], U32, align_bytes=64)
+        basis_scales = keep.tile([P, GROUPS * PACK * PASSES * P], U8, align_bytes=64)
+        coef_codes = keep.tile([P, HALVES, PASSES, 2, N], U32, align_bytes=64)
+        coef_scales = keep.tile([P, HALVES, PASSES, 2, N], U8, align_bytes=64)
+        y_scales = keep.tile([P, GROUPS, S], U8, align_bytes=64)
+
+        coef_grouped, basis_turned, basis_grouped = {}, {}, {}
+        acc, sq, total, y, y_grouped = {}, {}, {}, {}, {}
+
+        def load_coef(h, c, part):
+            rows = coefs[part][c * SPAN : (c + 1) * SPAN, h * N : (h + 1) * N]
+            nc.sync.dma_start(out=coef_raw[:, h, c, part], in_=rows.rearrange("(p j) s -> p j s", j=PACK))
+
+        def load_basis(g, t0, t1):
+            rows = basis[g * SPAN : (g + 1) * SPAN, :].rearrange("(p t) k -> p t k", t=PACK)
+            nc.sync.dma_start(out=basis_raw[:, g, t0:t1], in_=rows[:, t0:t1])
+
+        def interleave(dst, src, scalar_cols):
+            cut = N - scalar_cols
+            if cut > 0:
+                nc.vector.tensor_copy(
+                    out=dst[:, :cut].rearrange("p (c i) t -> p c t i", i=RUN),
+                    in_=src[:, :, :cut].rearrange("p t (c i) -> p c t i", i=RUN),
+                )
+            if cut < N:
+                nc.scalar.copy(
+                    out=dst[:, cut:].rearrange("p (c i) t -> p c t i", i=RUN),
+                    in_=src[:, :, cut:].rearrange("p t (c i) -> p c t i", i=RUN),
+                )
+
+        def group_coef(h, item):
+            c, part = divmod(item, 2)
+            grouped = stage.tile([P, N, PACK], BF16, align_bytes=64, name="coef_grouped")
+            coef_grouped[h, item] = grouped
+            interleave(grouped, coef_raw[:, h, c, part], COEF_SCALAR_COLS[h][item])
+
+        def quantize_coef(h, item):
+            c, part = divmod(item, 2)
+            nc.vector.quantize_mx(
+                out=coef_codes[:, h, c, part].bitcast(FP8X4),
+                scales=coef_scales[:, h, c, part],
+                in_=coef_grouped[h, item][:].rearrange("p n t -> p (n t)"),
+            )
+
+        def turn_basis(tiles):
+            for n in tiles:
+                g, t = divmod(n, PACK)
+                pairs = basis_raw[:, g, t].bitcast(F32)
+                turned = turn_psum.tile([P, PASSES, 2, P], F32, name="turned")
+                basis_turned[n] = turned
+                for c in range(PASSES):
+                    for u in range(2):
+                        nc.tensor.transpose(turned[:, c, u], pairs[:, 256 * c + u : 256 * (c + 1) : 2], ident[:])
+
+        def group_basis(tiles):
+            grouped = stage.tile([P, 2, PASSES, P, 2], F32, align_bytes=64, name="basis_grouped")
+            basis_grouped[tiles] = grouped
+            for j, n in enumerate(tiles):
+                nc.scalar.copy(out=grouped[:, j], in_=basis_turned[n][:].rearrange("p c u r -> p c r u"))
+
+        def quantize_basis(tiles):
+            cols = slice(tiles[0] * PASSES * P, (tiles[-1] + 1) * PASSES * P)
+            grouped = basis_grouped[tiles][:, : len(tiles)].rearrange("p j c r u -> p (j c r u)")
+            nc.vector.quantize_mx(
+                out=basis_codes[:, cols].bitcast(FP8X4), scales=basis_scales[:, cols], in_=grouped.bitcast(BF16)
+            )
+
+        def place(step):
+            unit, t = divmod(step, PACK)
+            g, h = divmod(unit, HALVES)
+            return unit, g, h, t
+
+        def multiply(step):
+            unit, g, h, t = place(step)
+            for part in range(2):
+                bank = acc_psum.tile([P, N], F32, name="acc%d" % part)
+                acc[step, part] = bank
+                for c in range(PASSES):
+                    col = ((g * PACK + t) * PASSES + c) * P
+                    nc.tensor.matmul_mx(
+                        out=bank[:],
+                        lhsT=basis_codes[:, col : col + P].bitcast(FP8X4),
+                        lhsT_scale=basis_scales[:, col : col + P],
+                        rhs=coef_codes[:, h, c, part].bitcast(FP8X4),
+                        rhs_scale=coef_scales[:, h, c, part],
+                        start=(c == 0),
+                        stop=(c == PASSES - 1),
+                    )
+
+        def square(step):
+            for part in range(2):
+                squared = squares.tile([P, N], F32, name="squared%d" % part)
+                sq[step, part] = squared
+                nc.scalar.activation(out=squared[:], in_=acc[step, part][:], func=SQUARE)
+
+        def add(step):
+            summed = stage.tile([P, N], F32, name="summed")
+            total[step] = summed
+            nc.vector.tensor_tensor(out=summed[:], in0=sq[step, 0][:], in1=sq[step, 1][:], op=ADD)
+
+        def weigh(step):
+            unit, g, h, t = place(step)
+            if t == 0:
+                y[unit] = stage.tile([P, PACK, N], F32, name="y")
+            nc.vector.tensor_scalar(
+                out=y[unit][:, t], in0=total[step][:], scalar1=jac_sb[:, g, t : t + 1], scalar2=None, op0=MULT
+            )
+            rows = out_0[g * SPAN : (g + 1) * SPAN, h * N : (h + 1) * N].rearrange("(p t) m -> p t m", t=PACK)
+            nc.sync.dma_start(out=rows[:, t], in_=y[unit][:, t])
+
+        def group_y(unit):
+            grouped = stage.tile([P, N, PACK], BF16, align_bytes=64, name="y_grouped")
+            y_grouped[unit] = grouped
+            interleave(grouped, y[unit], CAST_SCALAR_COLS[unit])
+
+        def store_scales(g0, g1, queues):
+            for q in range(4):
+                queues[q].dma_start(
+                    out=out_2[g0:g1, 4 * q : 4 * q + 4, :].rearrange("g r m -> r g m").bitcast(I32),
+                    in_=y_scales[32 * q : 32 * q + 4, g0:g1].bitcast(I32),
+                )
+
+        def quantize_y(unit):
+            g, h = divmod(unit, HALVES)
+            y_codes = stage.tile([P, N], U32, align_bytes=64, name="y_codes")
+            nc.vector.quantize_mx(
+                out=y_codes[:].bitcast(FP8X4),
+                scales=y_scales[:, g, h * N : (h + 1) * N],
+                in_=y_grouped[unit][:].rearrange("p n t -> p (n t)"),
+            )
+            nc.sync.dma_start(
+                out=out_1[g, :, h * N : (h + 1) * N, :].rearrange("p m t -> p (m t)").bitcast(I32),
+                in_=y_codes[:].bitcast(I32),
+            )
+            if unit == (GROUPS - 1) * HALVES - 1:
+                store_scales(0, GROUPS - 1, [nc.sync] * 4)
+            if unit == GROUPS * HALVES - 1:
+                store_scales(GROUPS - 1, GROUPS, [nc.scalar, nc.scalar, nc.sync, nc.sync])
+
+        nc.scalar.dma_start(out=jac_sb[:], in_=jac.rearrange("(g p t) -> p g t", g=GROUPS, t=PACK))
+        load_coef(0, 0, 0)
+        load_basis(0, 0, 1)
+        load_coef(0, 0, 1)
+        load_coef(0, 1, 0)
+        load_coef(0, 1, 1)
+        load_basis(0, 1, PACK)
+        for item in range(4):
+            load_coef(1, *divmod(item, 2))
+        for g in range(1, GROUPS):
+            load_basis(g, 0, PACK)
+        make_identity(nc, ident[:])
+
+        group_coef(0, 0)
+        turn_basis((0,))
+        group_basis((0,))
+        quantize_coef(0, 0)
+        group_coef(0, 1)
+        quantize_basis((0,))
+        group_coef(0, 2)
+        quantize_coef(0, 1)
+        group_coef(0, 3)
+        quantize_coef(0, 2)
+        turn_basis((1, 2))
+        quantize_coef(0, 3)
+        group_basis((1, 2))
+        group_coef(1, 0)
+        quantize_basis((1, 2))
+
+        for i in range(STEPS + LAG + 4):
+            g, within = divmod(i, HALVES * PACK)
+            tiles = ()
+            if i == 0:
+                tiles = (3,)
+            elif g < GROUPS - 1 and within in TURN_AT:
+                first = PACK * (g + 1) + 2 * TURN_AT.index(within)
+                tiles = (first, first + 1)
+            if i < STEPS:
+                multiply(i)
+                turn_basis(tiles)
+                square(i)
+                if tiles:
+                    group_basis(tiles)
+            if i == 0:
+                quantize_coef(1, 0)
+            if i < 3:
+                group_coef(1, i + 1)
+            if i == 0:
+                quantize_basis(tiles)
+            if 1 <= i < 3:
+                quantize_coef(1, i)
+            j = i - LAG
+            if 0 <= j < STEPS:
+                add(j)
+            if i == 2:
+                quantize_coef(1, 3)
+            if tiles and i > 0:
+                quantize_basis(tiles)
+            if 0 <= j - 1 < STEPS:
+                weigh(j - 1)
+            if 0 <= j - 2 < STEPS and (j - 2) % PACK == PACK - 1:
+                group_y((j - 2) // PACK)
+            if 0 <= j - 3 < STEPS and (j - 3) % PACK == PACK - 1:
+                quantize_y((j - 3) // PACK)

@@ -12,6 +12,7 @@ I32 = mybir.dt.int32
 U32 = mybir.dt.uint32
 U8 = mybir.dt.uint8
 FP8X4 = mybir.dt.float8_e4m3fn_x4
+COPY = mybir.ActivationFunctionType.Copy
 SQUARE = mybir.ActivationFunctionType.Square
 ADD = mybir.AluOpType.add
 MULT = mybir.AluOpType.mult
@@ -23,13 +24,18 @@ N = 512
 GROUPS = G // SPAN
 PASSES = K // SPAN
 HALVES = S // N
-STEPS = GROUPS * HALVES * PACK
-RUN = 4
+UNITS = (
+    (0, 0, N), (0, N, N), (1, 0, N), (1, N, N), (2, 0, N), (2, N, N), (3, 0, N),
+    (3, N, N // 2), (3, N + N // 2, N // 2),
+)
+STEPS = 9 * PACK
+COEF_RUN = 4
+Y_RUN = 4
 
-COEF_SCALAR_COLS = {0: (256, 256, 256, 256), 1: (0, 128, 128, 128)}
-CAST_SCALAR_COLS = (0, 0, 0, 0, 0, 192, 192, 192)
+COEF_SCALAR_COLS = {0: (192, 192, 256, 64), 1: (160, 160, 160, 160)}
+Y_SCALAR_COLS = (32, 32, 32, 32, 128, 192, 192, 128, 64)
+WEIGH_ON_SCALAR = (STEPS - 3, STEPS - 1)
 TURN_AT = (3, 5)
-LAG = 1
 
 
 def tile_hermite_state_density_g2_kernel(tc, basis, coef_re, coef_im, jac, out_0, out_1, out_2):
@@ -38,14 +44,14 @@ def tile_hermite_state_density_g2_kernel(tc, basis, coef_re, coef_im, jac, out_0
 
     with ExitStack() as ctx:
         keep = ctx.enter_context(tc.tile_pool(name="keep", bufs=1))
-        stage = ctx.enter_context(tc.tile_pool(name="stage", bufs=3))
+        stage = ctx.enter_context(tc.tile_pool(name="stage", bufs=4))
         squares = ctx.enter_context(tc.tile_pool(name="squares", bufs=8))
-        turn_psum = ctx.enter_context(tc.psum_pool(name="turn_psum", bufs=2))
-        acc_psum = ctx.enter_context(tc.psum_pool(name="acc_psum", bufs=3))
+        psum = ctx.enter_context(tc.psum_pool(name="psum", bufs=8))
         ctx.enter_context(tc.manual_schedule())
 
         ident = keep.tile([P, P], F32)
         jac_sb = keep.tile([P, GROUPS, PACK], BF16)
+        jac_f32 = keep.tile([P, GROUPS, PACK], F32)
         basis_raw = keep.tile([P, GROUPS, PACK, K], BF16)
         coef_raw = keep.tile([P, HALVES, PASSES, 2, PACK, N], BF16)
         basis_codes = keep.tile([P, GROUPS * PACK * PASSES * P], U32, align_bytes=64)
@@ -65,27 +71,23 @@ def tile_hermite_state_density_g2_kernel(tc, basis, coef_re, coef_im, jac, out_0
             rows = basis[g * SPAN : (g + 1) * SPAN, :].rearrange("(p t) k -> p t k", t=PACK)
             nc.sync.dma_start(out=basis_raw[:, g, t0:t1], in_=rows[:, t0:t1])
 
-        def interleave(dst, src, scalar_cols):
-            cut = N - scalar_cols
-            if cut > 0:
-                nc.vector.tensor_copy(
-                    out=dst[:, :cut].rearrange("p (c i) t -> p c t i", i=RUN),
-                    in_=src[:, :, :cut].rearrange("p t (c i) -> p c t i", i=RUN),
-                )
-            if cut < N:
-                nc.scalar.copy(
-                    out=dst[:, cut:].rearrange("p (c i) t -> p c t i", i=RUN),
-                    in_=src[:, :, cut:].rearrange("p t (c i) -> p c t i", i=RUN),
+        def interleave(copy, dst, src, cols, run):
+            if cols.start < cols.stop:
+                copy(
+                    out=dst[:, cols].rearrange("p (c i) t -> p c t i", i=run),
+                    in_=src[:, :, cols].rearrange("p t (c i) -> p c t i", i=run),
                 )
 
         def group_coef(h, item):
-            c, part = divmod(item, 2)
+            part, c = divmod(item, PASSES)
             grouped = stage.tile([P, N, PACK], BF16, align_bytes=64, name="coef_grouped")
             coef_grouped[h, item] = grouped
-            interleave(grouped, coef_raw[:, h, c, part], COEF_SCALAR_COLS[h][item])
+            cut = N - COEF_SCALAR_COLS[h][item]
+            interleave(nc.vector.tensor_copy, grouped, coef_raw[:, h, c, part], slice(0, cut), COEF_RUN)
+            interleave(nc.scalar.copy, grouped, coef_raw[:, h, c, part], slice(cut, N), COEF_RUN)
 
         def quantize_coef(h, item):
-            c, part = divmod(item, 2)
+            part, c = divmod(item, PASSES)
             nc.vector.quantize_mx(
                 out=coef_codes[:, h, c, part].bitcast(FP8X4),
                 scales=coef_scales[:, h, c, part],
@@ -96,7 +98,7 @@ def tile_hermite_state_density_g2_kernel(tc, basis, coef_re, coef_im, jac, out_0
             for n in tiles:
                 g, t = divmod(n, PACK)
                 pairs = basis_raw[:, g, t].bitcast(F32)
-                turned = turn_psum.tile([P, PASSES, 2, P], F32, name="turned")
+                turned = psum.tile([P, PASSES, 2, P], F32, name="bank")
                 basis_turned[n] = turned
                 for c in range(PASSES):
                     for u in range(2):
@@ -115,53 +117,59 @@ def tile_hermite_state_density_g2_kernel(tc, basis, coef_re, coef_im, jac, out_0
                 out=basis_codes[:, cols].bitcast(FP8X4), scales=basis_scales[:, cols], in_=grouped.bitcast(BF16)
             )
 
-        def place(step):
+        def multiply(step, part):
             unit, t = divmod(step, PACK)
-            g, h = divmod(unit, HALVES)
-            return unit, g, h, t
+            g, col0, width = UNITS[unit]
+            h, lo = divmod(col0, N)
+            bank = psum.tile([P, width], F32, name="bank")
+            acc[step, part] = bank
+            for c in range(PASSES):
+                col = ((g * PACK + t) * PASSES + c) * P
+                nc.tensor.matmul_mx(
+                    out=bank[:],
+                    lhsT=basis_codes[:, col : col + P].bitcast(FP8X4),
+                    lhsT_scale=basis_scales[:, col : col + P],
+                    rhs=coef_codes[:, h, c, part, lo : lo + width].bitcast(FP8X4),
+                    rhs_scale=coef_scales[:, h, c, part, lo : lo + width],
+                    start=(c == 0),
+                    stop=(c == PASSES - 1),
+                )
 
-        def multiply(step):
-            unit, g, h, t = place(step)
-            for part in range(2):
-                bank = acc_psum.tile([P, N], F32, name="acc%d" % part)
-                acc[step, part] = bank
-                for c in range(PASSES):
-                    col = ((g * PACK + t) * PASSES + c) * P
-                    nc.tensor.matmul_mx(
-                        out=bank[:],
-                        lhsT=basis_codes[:, col : col + P].bitcast(FP8X4),
-                        lhsT_scale=basis_scales[:, col : col + P],
-                        rhs=coef_codes[:, h, c, part].bitcast(FP8X4),
-                        rhs_scale=coef_scales[:, h, c, part],
-                        start=(c == 0),
-                        stop=(c == PASSES - 1),
-                    )
-
-        def square(step):
-            for part in range(2):
-                squared = squares.tile([P, N], F32, name="squared%d" % part)
-                sq[step, part] = squared
-                nc.scalar.activation(out=squared[:], in_=acc[step, part][:], func=SQUARE)
+        def square(step, part):
+            squared = squares.tile([P, UNITS[step // PACK][2]], F32, name="squared%d" % part)
+            sq[step, part] = squared
+            nc.scalar.activation(out=squared[:], in_=acc[step, part][:], func=SQUARE)
 
         def add(step):
-            summed = stage.tile([P, N], F32, name="summed")
+            summed = stage.tile([P, UNITS[step // PACK][2]], F32, name="summed")
             total[step] = summed
             nc.vector.tensor_tensor(out=summed[:], in0=sq[step, 0][:], in1=sq[step, 1][:], op=ADD)
 
         def weigh(step):
-            unit, g, h, t = place(step)
+            unit, t = divmod(step, PACK)
+            g, col0, width = UNITS[unit]
             if t == 0:
-                y[unit] = stage.tile([P, PACK, N], F32, name="y")
-            nc.vector.tensor_scalar(
-                out=y[unit][:, t], in0=total[step][:], scalar1=jac_sb[:, g, t : t + 1], scalar2=None, op0=MULT
-            )
-            rows = out_0[g * SPAN : (g + 1) * SPAN, h * N : (h + 1) * N].rearrange("(p t) m -> p t m", t=PACK)
-            nc.sync.dma_start(out=rows[:, t], in_=y[unit][:, t])
+                y[unit] = stage.tile([P, PACK, width], F32, name="y")
+            if step in WEIGH_ON_SCALAR:
+                nc.scalar.activation(out=y[unit][:, t], in_=total[step][:], func=COPY, scale=jac_f32[:, g, t : t + 1])
+            else:
+                nc.vector.tensor_scalar(
+                    out=y[unit][:, t], in0=total[step][:], scalar1=jac_sb[:, g, t : t + 1], scalar2=None, op0=MULT
+                )
+            rows = out_0[g * SPAN : (g + 1) * SPAN, col0 : col0 + width].rearrange("(p t) m -> p t m", t=PACK)
+            together = N // width
+            if (t + 1) % together == 0:
+                nc.sync.dma_start(out=rows[:, t + 1 - together : t + 1], in_=y[unit][:, t + 1 - together : t + 1])
 
-        def group_y(unit):
-            grouped = stage.tile([P, N, PACK], BF16, align_bytes=64, name="y_grouped")
+        def group_y_vector(unit):
+            width = UNITS[unit][2]
+            grouped = stage.tile([P, width, PACK], BF16, align_bytes=64, name="y_grouped")
             y_grouped[unit] = grouped
-            interleave(grouped, y[unit], CAST_SCALAR_COLS[unit])
+            interleave(nc.vector.tensor_copy, grouped, y[unit], slice(0, width - Y_SCALAR_COLS[unit]), Y_RUN)
+
+        def group_y_scalar(unit):
+            width = UNITS[unit][2]
+            interleave(nc.scalar.copy, y_grouped[unit], y[unit], slice(width - Y_SCALAR_COLS[unit], width), Y_RUN)
 
         def store_scales(g0, g1, queues):
             for q in range(4):
@@ -171,31 +179,33 @@ def tile_hermite_state_density_g2_kernel(tc, basis, coef_re, coef_im, jac, out_0
                 )
 
         def quantize_y(unit):
-            g, h = divmod(unit, HALVES)
-            y_codes = stage.tile([P, N], U32, align_bytes=64, name="y_codes")
+            g, col0, width = UNITS[unit]
+            y_codes = stage.tile([P, width], U32, align_bytes=64, name="y_codes")
             nc.vector.quantize_mx(
                 out=y_codes[:].bitcast(FP8X4),
-                scales=y_scales[:, g, h * N : (h + 1) * N],
+                scales=y_scales[:, g, col0 : col0 + width],
                 in_=y_grouped[unit][:].rearrange("p n t -> p (n t)"),
             )
             nc.sync.dma_start(
-                out=out_1[g, :, h * N : (h + 1) * N, :].rearrange("p m t -> p (m t)").bitcast(I32),
+                out=out_1[g, :, col0 : col0 + width, :].rearrange("p m t -> p (m t)").bitcast(I32),
                 in_=y_codes[:].bitcast(I32),
             )
             if unit == (GROUPS - 1) * HALVES - 1:
                 store_scales(0, GROUPS - 1, [nc.sync] * 4)
-            if unit == GROUPS * HALVES - 1:
+            if unit == len(UNITS) - 1:
                 store_scales(GROUPS - 1, GROUPS, [nc.scalar, nc.scalar, nc.sync, nc.sync])
 
-        nc.scalar.dma_start(out=jac_sb[:], in_=jac.rearrange("(g p t) -> p g t", g=GROUPS, t=PACK))
         load_coef(0, 0, 0)
         load_basis(0, 0, 1)
-        load_coef(0, 0, 1)
         load_coef(0, 1, 0)
+        load_basis(0, 1, 2)
+        load_coef(0, 0, 1)
         load_coef(0, 1, 1)
-        load_basis(0, 1, PACK)
-        for item in range(4):
-            load_coef(1, *divmod(item, 2))
+        load_basis(0, 2, PACK)
+        for part in range(2):
+            for c in range(PASSES):
+                load_coef(1, c, part)
+        nc.sync.dma_start(out=jac_sb[:], in_=jac.rearrange("(g p t) -> p g t", g=GROUPS, t=PACK))
         for g in range(1, GROUPS):
             load_basis(g, 0, PACK)
         make_identity(nc, ident[:])
@@ -206,48 +216,59 @@ def tile_hermite_state_density_g2_kernel(tc, basis, coef_re, coef_im, jac, out_0
         quantize_coef(0, 0)
         group_coef(0, 1)
         quantize_basis((0,))
-        group_coef(0, 2)
+        turn_basis((1,))
+        group_basis((1,))
         quantize_coef(0, 1)
+        group_coef(0, 2)
+        quantize_basis((1,))
+        multiply(0, 0)
+        square(0, 0)
+        multiply(1, 0)
         group_coef(0, 3)
+        square(1, 0)
         quantize_coef(0, 2)
-        turn_basis((1, 2))
+        turn_basis((2, 3))
         quantize_coef(0, 3)
-        group_basis((1, 2))
-        group_coef(1, 0)
-        quantize_basis((1, 2))
+        group_basis((2, 3))
 
-        for i in range(STEPS + LAG + 4):
+        for i in range(STEPS + 4):
             g, within = divmod(i, HALVES * PACK)
             tiles = ()
-            if i == 0:
-                tiles = (3,)
-            elif g < GROUPS - 1 and within in TURN_AT:
+            if g < GROUPS - 1 and within in TURN_AT:
                 first = PACK * (g + 1) + 2 * TURN_AT.index(within)
                 tiles = (first, first + 1)
             if i < STEPS:
-                multiply(i)
+                parts = (1,) if i < 2 else (0, 1)
+                for part in parts:
+                    multiply(i, part)
                 turn_basis(tiles)
-                square(i)
+                for part in parts:
+                    square(i, part)
                 if tiles:
                     group_basis(tiles)
             if i == 0:
-                quantize_coef(1, 0)
-            if i < 3:
-                group_coef(1, i + 1)
-            if i == 0:
-                quantize_basis(tiles)
-            if 1 <= i < 3:
-                quantize_coef(1, i)
-            j = i - LAG
-            if 0 <= j < STEPS:
-                add(j)
-            if i == 2:
+                quantize_basis((2, 3))
+            if i < 2:
+                for item in (2 * i, 2 * i + 1):
+                    group_coef(1, item)
+                    if item > 0:
+                        quantize_coef(1, item - 1)
+            if i == HALVES * PACK:
+                nc.scalar.copy(out=jac_f32[:], in_=jac_sb[:])
+            if 1 <= i <= STEPS:
+                add(i - 1)
+            if i == 1:
                 quantize_coef(1, 3)
-            if tiles and i > 0:
+            if tiles:
                 quantize_basis(tiles)
-            if 0 <= j - 1 < STEPS:
-                weigh(j - 1)
-            if 0 <= j - 2 < STEPS and (j - 2) % PACK == PACK - 1:
-                group_y((j - 2) // PACK)
-            if 0 <= j - 3 < STEPS and (j - 3) % PACK == PACK - 1:
-                quantize_y((j - 3) // PACK)
+            if 2 <= i <= STEPS + 1:
+                weigh(i - 2)
+            for unit in range(len(UNITS)):
+                done = PACK * unit + PACK + 2
+                delay = 1 if unit < len(UNITS) - 1 else 0
+                if i == done:
+                    group_y_vector(unit)
+                if i == done + delay:
+                    group_y_scalar(unit)
+                if i == done + delay + 1:
+                    quantize_y(unit)

@@ -30,7 +30,7 @@ UNITS = (
 )
 STEPS = 9 * PACK
 COEF_RUN = 4
-Y_RUN = 4
+Y_RUN = 2
 
 COEF_SCALAR_COLS = {0: (192, 192, 256, 64), 1: (160, 160, 160, 160)}
 Y_SCALAR_COLS = (32, 32, 32, 32, 128, 192, 192, 128, 64)

@@ -25,17 +25,18 @@ GROUPS = G // SPAN
 PASSES = K // SPAN
 HALVES = S // N
 UNITS = (
-    (0, 0, N), (0, N, N), (1, 0, N), (1, N, N), (2, 0, N), (2, N, N), (3, 0, N),
-    (3, N, N // 2), (3, N + N // 2, N // 2),
+    (0, 0, N), (1, 0, N), (0, N, N), (1, N, N), (2, 0, N), (2, N, N), (3, 0, N),
+    (3, N, N),
 )
-STEPS = 9 * PACK
+STEPS = 8 * PACK
 COEF_RUN = 4
 Y_RUN = 2
 
-COEF_SCALAR_COLS = {0: (192, 192, 256, 64), 1: (160, 160, 160, 160)}
-Y_SCALAR_COLS = (32, 32, 32, 32, 128, 192, 192, 128, 64)
-WEIGH_ON_SCALAR = (STEPS - 3, STEPS - 1)
-TURN_AT = (3, 5)
+COEF_SCALAR_COLS = {0: (192, 192, 256, 64), 1: (128, 128, 128, 128)}
+Y_SCALAR_COLS = (32, 32, 32, 32, 128, 192, 192, 192)
+WEIGH_ON_SCALAR = (STEPS - 2,)
+TURN_AT = (2, 3, 13, 15, 17, 19)
+GROUP_COEF_AT = (0, 2, 3, 4)
 
 
 def tile_hermite_state_density_g2_kernel(tc, basis, coef_re, coef_im, jac, out_0, out_1, out_2):
@@ -202,11 +203,14 @@ def tile_hermite_state_density_g2_kernel(tc, basis, coef_re, coef_im, jac, out_0
         load_coef(0, 0, 1)
         load_coef(0, 1, 1)
         load_basis(0, 2, PACK)
-        for part in range(2):
-            for c in range(PASSES):
-                load_coef(1, c, part)
+        load_basis(1, 0, 2)
+        load_coef(1, 0, 0)
         nc.sync.dma_start(out=jac_sb[:], in_=jac.rearrange("(g p t) -> p g t", g=GROUPS, t=PACK))
-        for g in range(1, GROUPS):
+        load_coef(1, 1, 0)
+        load_basis(1, 2, PACK)
+        load_coef(1, 0, 1)
+        load_coef(1, 1, 1)
+        for g in range(2, GROUPS):
             load_basis(g, 0, PACK)
         make_identity(nc, ident[:])
 
@@ -232,10 +236,9 @@ def tile_hermite_state_density_g2_kernel(tc, basis, coef_re, coef_im, jac, out_0
         group_basis((2, 3))
 
         for i in range(STEPS + 4):
-            g, within = divmod(i, HALVES * PACK)
             tiles = ()
-            if g < GROUPS - 1 and within in TURN_AT:
-                first = PACK * (g + 1) + 2 * TURN_AT.index(within)
+            if i in TURN_AT:
+                first = PACK + 2 * TURN_AT.index(i)
                 tiles = (first, first + 1)
             if i < STEPS:
                 parts = (1,) if i < 2 else (0, 1)
@@ -248,16 +251,16 @@ def tile_hermite_state_density_g2_kernel(tc, basis, coef_re, coef_im, jac, out_0
                     group_basis(tiles)
             if i == 0:
                 quantize_basis((2, 3))
-            if i < 2:
-                for item in (2 * i, 2 * i + 1):
-                    group_coef(1, item)
-                    if item > 0:
-                        quantize_coef(1, item - 1)
+            if i in GROUP_COEF_AT:
+                item = GROUP_COEF_AT.index(i)
+                group_coef(1, item)
+                if item > 0:
+                    quantize_coef(1, item - 1)
             if i == HALVES * PACK:
                 nc.scalar.copy(out=jac_f32[:], in_=jac_sb[:])
             if 1 <= i <= STEPS:
                 add(i - 1)
-            if i == 1:
+            if i == GROUP_COEF_AT[-1]:
                 quantize_coef(1, 3)
             if tiles:
                 quantize_basis(tiles)

from contextlib import ExitStack

import concourse.mybir as mybir
from concourse.masks import make_identity

G, K, S = 2048, 1024, 1024
FLOPS = 2 * 2 * G * K * S

F32 = mybir.dt.float32
BF16 = mybir.dt.bfloat16
I32 = mybir.dt.int32
U32 = mybir.dt.uint32
U8 = mybir.dt.uint8
FP8X4 = mybir.dt.float8_e4m3fn_x4
COPY = mybir.ActivationFunctionType.Copy
SQUARE = mybir.ActivationFunctionType.Square
ADD = mybir.AluOpType.add
MULT = mybir.AluOpType.mult

P = 128
PACK = 4
SPAN = P * PACK
N = 512
GROUPS = G // SPAN
PASSES = K // SPAN
HALVES = S // N
UNITS = (
    (0, 0, N), (1, 0, N), (0, N, N), (1, N, N), (2, 0, N), (2, N, N), (3, 0, N),
    (3, N, N),
)
STEPS = 8 * PACK
COEF_RUN = 4
Y_RUN = 2

COEF_SCALAR_COLS = {0: (192, 192, 256, 64), 1: (128, 128, 128, 128)}
Y_SCALAR_COLS = (32, 32, 32, 32, 128, 192, 192, 192)
WEIGH_ON_SCALAR = (STEPS - 2,)
TURN_AT = (2, 3, 13, 15, 17, 19)
GROUP_COEF_AT = (0, 2, 3, 4)


def tile_hermite_state_density_g2_kernel(tc, basis, coef_re, coef_im, jac, out_0, out_1, out_2):
    nc = tc.nc
    coefs = (coef_re, coef_im)

    with ExitStack() as ctx:
        keep = ctx.enter_context(tc.tile_pool(name="keep", bufs=1))
        stage = ctx.enter_context(tc.tile_pool(name="stage", bufs=4))
        squares = ctx.enter_context(tc.tile_pool(name="squares", bufs=8))
        psum = ctx.enter_context(tc.psum_pool(name="psum", bufs=8))
        ctx.enter_context(tc.manual_schedule())

        ident = keep.tile([P, P], F32)
        jac_sb = keep.tile([P, GROUPS, PACK], BF16)
        jac_f32 = keep.tile([P, GROUPS, PACK], F32)
        basis_raw = keep.tile([P, GROUPS, PACK, K], BF16)
        coef_raw = keep.tile([P, HALVES, PASSES, 2, PACK, N], BF16)
        basis_codes = keep.tile([P, GROUPS * PACK * PASSES * P], U32, align_bytes=64)
        basis_scales = keep.tile([P, GROUPS * PACK * PASSES * P], U8, align_bytes=64)
        coef_codes = keep.tile([P, HALVES, PASSES, 2, N], U32, align_bytes=64)
        coef_scales = keep.tile([P, HALVES, PASSES, 2, N], U8, align_bytes=64)
        y_scales = keep.tile([P, GROUPS, S], U8, align_bytes=64)

        coef_grouped, basis_turned, basis_grouped = {}, {}, {}
        acc, sq, total, y, y_grouped = {}, {}, {}, {}, {}

        def load_coef(h, c, part):
            rows = coefs[part][c * SPAN : (c + 1) * SPAN, h * N : (h + 1) * N]
            nc.sync.dma_start(out=coef_raw[:, h, c, part], in_=rows.rearrange("(p j) s -> p j s", j=PACK))

        def load_basis(g, t0, t1):
            rows = basis[g * SPAN : (g + 1) * SPAN, :].rearrange("(p t) k -> p t k", t=PACK)
            nc.sync.dma_start(out=basis_raw[:, g, t0:t1], in_=rows[:, t0:t1])

        def interleave(copy, dst, src, cols, run):
            if cols.start < cols.stop:
                copy(
                    out=dst[:, cols].rearrange("p (c i) t -> p c t i", i=run),
                    in_=src[:, :, cols].rearrange("p t (c i) -> p c t i", i=run),
                )

        def group_coef(h, item):
            part, c = divmod(item, PASSES)
            grouped = stage.tile([P, N, PACK], BF16, align_bytes=64, name="coef_grouped")
            coef_grouped[h, item] = grouped
            cut = N - COEF_SCALAR_COLS[h][item]
            interleave(nc.vector.tensor_copy, grouped, coef_raw[:, h, c, part], slice(0, cut), COEF_RUN)
            interleave(nc.scalar.copy, grouped, coef_raw[:, h, c, part], slice(cut, N), COEF_RUN)

        def quantize_coef(h, item):
            part, c = divmod(item, PASSES)
            nc.vector.quantize_mx(
                out=coef_codes[:, h, c, part].bitcast(FP8X4),
                scales=coef_scales[:, h, c, part],
                in_=coef_grouped[h, item][:].rearrange("p n t -> p (n t)"),
            )

        def turn_basis(tiles):
            for n in tiles:
                g, t = divmod(n, PACK)
                pairs = basis_raw[:, g, t].bitcast(F32)
                turned = psum.tile([P, PASSES, 2, P], F32, name="bank")
                basis_turned[n] = turned
                for c in range(PASSES):
                    for u in range(2):
                        nc.tensor.transpose(turned[:, c, u], pairs[:, 256 * c + u : 256 * (c + 1) : 2], ident[:])

        def group_basis(tiles):
            grouped = stage.tile([P, 2, PASSES, P, 2], F32, align_bytes=64, name="basis_grouped")
            basis_grouped[tiles] = grouped
            for j, n in enumerate(tiles):
                nc.scalar.copy(out=grouped[:, j], in_=basis_turned[n][:].rearrange("p c u r -> p c r u"))

        def quantize_basis(tiles):
            cols = slice(tiles[0] * PASSES * P, (tiles[-1] + 1) * PASSES * P)
            grouped = basis_grouped[tiles][:, : len(tiles)].rearrange("p j c r u -> p (j c r u)")
            nc.vector.quantize_mx(
                out=basis_codes[:, cols].bitcast(FP8X4), scales=basis_scales[:, cols], in_=grouped.bitcast(BF16)
            )

        def multiply(step, part):
            unit, t = divmod(step, PACK)
            g, col0, width = UNITS[unit]
            h, lo = divmod(col0, N)
            bank = psum.tile([P, width], F32, name="bank")
            acc[step, part] = bank
            for c in range(PASSES):
                col = ((g * PACK + t) * PASSES + c) * P
                nc.tensor.matmul_mx(
                    out=bank[:],
                    lhsT=basis_codes[:, col : col + P].bitcast(FP8X4),
                    lhsT_scale=basis_scales[:, col : col + P],
                    rhs=coef_codes[:, h, c, part, lo : lo + width].bitcast(FP8X4),
                    rhs_scale=coef_scales[:, h, c, part, lo : lo + width],
                    start=(c == 0),
                    stop=(c == PASSES - 1),
                )

        def square(step, part):
            squared = squares.tile([P, UNITS[step // PACK][2]], F32, name="squared%d" % part)
            sq[step, part] = squared
            nc.scalar.activation(out=squared[:], in_=acc[step, part][:], func=SQUARE)

        def add(step):
            summed = stage.tile([P, UNITS[step // PACK][2]], F32, name="summed")
            total[step] = summed
            nc.vector.tensor_tensor(out=summed[:], in0=sq[step, 0][:], in1=sq[step, 1][:], op=ADD)

        def weigh(step):
            unit, t = divmod(step, PACK)
            g, col0, width = UNITS[unit]
            if t == 0:
                y[unit] = stage.tile([P, PACK, width], F32, name="y")
            if step in WEIGH_ON_SCALAR:
                nc.scalar.activation(out=y[unit][:, t], in_=total[step][:], func=COPY, scale=jac_f32[:, g, t : t + 1])
            else:
                nc.vector.tensor_scalar(
                    out=y[unit][:, t], in0=total[step][:], scalar1=jac_sb[:, g, t : t + 1], scalar2=None, op0=MULT
                )
            rows = out_0[g * SPAN : (g + 1) * SPAN, col0 : col0 + width].rearrange("(p t) m -> p t m", t=PACK)
            together = N // width
            if (t + 1) % together == 0:
                nc.sync.dma_start(out=rows[:, t + 1 - together : t + 1], in_=y[unit][:, t + 1 - together : t + 1])

        def group_y_vector(unit):
            width = UNITS[unit][2]
            grouped = stage.tile([P, width, PACK], BF16, align_bytes=64, name="y_grouped")
            y_grouped[unit] = grouped
            interleave(nc.vector.tensor_copy, grouped, y[unit], slice(0, width - Y_SCALAR_COLS[unit]), Y_RUN)

        def group_y_scalar(unit):
            width = UNITS[unit][2]
            interleave(nc.scalar.copy, y_grouped[unit], y[unit], slice(width - Y_SCALAR_COLS[unit], width), Y_RUN)

        def store_scales(g0, g1, queues):
            for q in range(4):
                queues[q].dma_start(
                    out=out_2[g0:g1, 4 * q : 4 * q + 4, :].rearrange("g r m -> r g m").bitcast(I32),
                    in_=y_scales[32 * q : 32 * q + 4, g0:g1].bitcast(I32),
                )

        def quantize_y(unit):
            g, col0, width = UNITS[unit]
            y_codes = stage.tile([P, width], U32, align_bytes=64, name="y_codes")
            nc.vector.quantize_mx(
                out=y_codes[:].bitcast(FP8X4),
                scales=y_scales[:, g, col0 : col0 + width],
                in_=y_grouped[unit][:].rearrange("p n t -> p (n t)"),
            )
            nc.sync.dma_start(
                out=out_1[g, :, col0 : col0 + width, :].rearrange("p m t -> p (m t)").bitcast(I32),
                in_=y_codes[:].bitcast(I32),
            )
            if unit == (GROUPS - 1) * HALVES - 1:
                store_scales(0, GROUPS - 1, [nc.sync] * 4)
            if unit == len(UNITS) - 1:
                store_scales(GROUPS - 1, GROUPS, [nc.scalar, nc.scalar, nc.sync, nc.sync])

        load_coef(0, 0, 0)
        load_basis(0, 0, 1)
        load_coef(0, 1, 0)
        load_basis(0, 1, 2)
        load_coef(0, 0, 1)
        load_coef(0, 1, 1)
        load_basis(0, 2, PACK)
        load_basis(1, 0, 2)
        load_coef(1, 0, 0)
        nc.sync.dma_start(out=jac_sb[:], in_=jac.rearrange("(g p t) -> p g t", g=GROUPS, t=PACK))
        load_coef(1, 1, 0)
        load_basis(1, 2, PACK)
        load_coef(1, 0, 1)
        load_coef(1, 1, 1)
        for g in range(2, GROUPS):
            load_basis(g, 0, PACK)
        make_identity(nc, ident[:])

        group_coef(0, 0)
        turn_basis((0,))
        group_basis((0,))
        quantize_coef(0, 0)
        group_coef(0, 1)
        quantize_basis((0,))
        turn_basis((1,))
        group_basis((1,))
        quantize_coef(0, 1)
        group_coef(0, 2)
        quantize_basis((1,))
        multiply(0, 0)
        square(0, 0)
        multiply(1, 0)
        group_coef(0, 3)
        square(1, 0)
        quantize_coef(0, 2)
        turn_basis((2, 3))
        quantize_coef(0, 3)
        group_basis((2, 3))

        for i in range(STEPS + 4):
            tiles = ()
            if i in TURN_AT:
                first = PACK + 2 * TURN_AT.index(i)
                tiles = (first, first + 1)
            if i < STEPS:
                parts = (1,) if i < 2 else (0, 1)
                for part in parts:
                    multiply(i, part)
                turn_basis(tiles)
                for part in parts:
                    square(i, part)
                if tiles:
                    group_basis(tiles)
            if i == 0:
                quantize_basis((2, 3))
            if i in GROUP_COEF_AT:
                item = GROUP_COEF_AT.index(i)
                group_coef(1, item)
                if item > 0:
                    quantize_coef(1, item - 1)
            if i == HALVES * PACK:
                nc.scalar.copy(out=jac_f32[:], in_=jac_sb[:])
            if 1 <= i <= STEPS:
                add(i - 1)
            if i == GROUP_COEF_AT[-1]:
                quantize_coef(1, 3)
            if tiles:
                quantize_basis(tiles)
            if 2 <= i <= STEPS + 1:
                weigh(i - 2)
            for unit in range(len(UNITS)):
                done = PACK * unit + PACK + 2
                delay = 1 if unit < len(UNITS) - 1 else 0
                if i == done:
                    group_y_vector(unit)
                if i == done + delay:
                    group_y_scalar(unit)
                if i == done + delay + 1:
                    quantize_y(unit)
